import numpy as np
import ml_dtypes


def mxq(x, axis, fmt="e4m3"):
    dtype, down = {"e4m3": (ml_dtypes.float8_e4m3fn, 7), "e5m2": (ml_dtypes.float8_e5m2, 14)}[fmt]
    v = np.moveaxis(np.asarray(x, np.float32).astype(ml_dtypes.bfloat16).astype(np.float64), axis, -1)
    blocks = v.reshape(v.shape[:-1] + (-1, 32))
    amax = np.abs(blocks).max(-1, keepdims=True)
    byte = np.maximum(np.where(amax > 0, np.frexp(amax)[1] - 1 + 127, 0) - down, 1)
    scale = np.exp2(byte - 127.0)
    codes = (blocks / scale).astype(np.float32).astype(dtype).astype(np.float64)
    return np.moveaxis((codes * scale).reshape(v.shape), -1, axis)


WIDE = False


def mx_kscale(k):
    if not WIDE:
        return np.ones(k)
    levels = np.array([10, -10, 5, -5, 0])
    if k % 512:
        return np.exp2(np.random.permutation(np.resize(levels, k // 32))).repeat(32)
    a = np.empty((k // 512, 16))
    for p in range(k // 512):
        a[p, :8] = np.random.permutation(np.resize(levels, 8))
        for g in range(8):
            far = levels[np.abs(levels - a[p, g]) >= 10]
            a[p, g + 8] = far[np.random.randint(len(far))]
    return np.exp2(a.ravel()).repeat(32)


BF16 = ml_dtypes.bfloat16


def bf(x):
    return np.asarray(x, np.float32).astype(BF16)


def f64(x):
    return np.asarray(x).astype(np.float64)


E2M1 = np.array([0.0, 0.5, 1.0, 1.5, 2.0, 3.0, 4.0, 6.0, -0.0, -0.5, -1.0, -1.5, -2.0, -3.0, -4.0, -6.0])


def pack_weight(w, fmt):
    k, n = w.shape
    w = f64(bf(w)).reshape(k // 32, 32, n)
    amax = np.abs(w).max(1)
    if fmt == "e4m3":
        byte = np.frexp(amax)[1] - 1 + 127 - 7
    else:
        mant, ex = np.frexp(amax / 6.0)
        byte = np.where(mant > 0.5, ex, ex - 1) + 127
    byte = np.clip(np.where(amax > 0, byte, 1), 1, 254)
    scaled = (w * np.exp2(127.0 - byte)[:, None, :]).reshape(k, n).astype(np.float32)
    by_word = np.ascontiguousarray(scaled.reshape(k // 512, 128, 4, n).transpose(0, 1, 3, 2))
    if fmt == "e4m3":
        words = by_word.astype(ml_dtypes.float8_e4m3fn).view(np.uint8)
    else:
        c = by_word.astype(ml_dtypes.float4_e2m1fn).view(np.uint8) & 0xF
        words = c[..., 0::2] | (c[..., 1::2] << 4)
    return np.ascontiguousarray(words), np.ascontiguousarray(byte.astype(np.uint8).reshape(k // 512, 16, n))


def unpack_weight(words, scales, fmt):
    g, p, n, _ = words.shape
    if fmt == "e4m3":
        vals = np.ascontiguousarray(words).view(ml_dtypes.float8_e4m3fn).astype(np.float64)
    else:
        nib = np.empty((g, p, n, 4), np.uint8)
        nib[..., 0::2] = words & 0xF
        nib[..., 1::2] = words >> 4
        vals = E2M1[nib]
    vals = vals * np.repeat(np.exp2(scales.astype(np.float64) - 127.0), 8, axis=1)[..., None]
    return vals.transpose(0, 1, 3, 2).reshape(g * 512, n)
def pack4(w):
    words, scales = pack_weight(w, "e2m1")
    return words.reshape(words.shape[0], 128, -1), scales


def unpack4(words, scales):
    return unpack_weight(words.reshape(words.shape[0], 128, -1, 2), scales, "e2m1")


G, C, D, H, P = 4, 1024, 512, 1024, 512


def setup_inputs():
    s = mx_kscale(D)
    t = mx_kscale(C)
    models = 2.0 * np.random.standard_normal((G, D, H)) / np.sqrt(D) / s[:, None]
    desc = np.random.standard_normal((G, C, P)) / np.sqrt(C) / t[:, None]
    models_words, models_scales = pack4(models.reshape(G * D, H))
    desc_words, desc_scales = pack4(desc.reshape(G * C, P))
    return {"x": bf(np.random.standard_normal((G, C, D)) * s),
            "models_words": models_words, "models_scales": models_scales,
            "conf": bf(np.random.uniform(0.5, 1.5, (G, C)) * t),
            "desc_words": desc_words, "desc_scales": desc_scales}


def reference(x, models_words, models_scales, conf, desc_words, desc_scales):
    models = unpack4(models_words, models_scales).reshape(G, D, H)
    desc = unpack4(desc_words, desc_scales).reshape(G, C, P)
    r = mxq(f64(x), 2, "e4m3") @ models
    w = f64(conf)[:, :, None] / (1.0 + np.square(r))
    return mxq(w, 1, "e4m3").swapaxes(1, 2) @ desc

@@ -1,0 +1,301 @@
+from contextlib import ExitStack
+
+import concourse.mybir as mybir
+from concourse.masks import make_identity
+
+G, C, D, H, P = 4, 1024, 512, 1024, 512
+FLOPS = 2 * G * C * D * H + 2 * G * C * H * P
+
+F32 = mybir.dt.float32
+BF16 = mybir.dt.bfloat16
+I32 = mybir.dt.int32
+U32 = mybir.dt.uint32
+U8 = mybir.dt.uint8
+FP8X4 = mybir.dt.float8_e4m3fn_x4
+FP4X4 = mybir.dt.float4_e2m1fn_x4
+ACT = mybir.ActivationFunctionType
+ALU = mybir.AluOpType
+
+
+def tile_cauchy_hypothesis_pooling_s14_kernel(
+    tc, x, models_words, models_scales, conf, desc_words, desc_scales, out
+):
+    nc = tc.nc
+    with ExitStack() as ctx:
+        keep = ctx.enter_context(tc.tile_pool(name="keep", bufs=1))
+        work = ctx.enter_context(tc.tile_pool(name="work", bufs=2))
+        psum = ctx.enter_context(tc.psum_pool(name="psum", bufs=1))
+        ctx.enter_context(tc.manual_schedule())
+
+        as0 = keep.tile([128, 1024], U8, name="as0", align_bytes=64)
+        asr = keep.tile([128, 3, 1024], U8, name="asr", align_bytes=64)
+        zs = keep.tile([128, 8, 512], U8, name="zs", align_bytes=64)
+        one = keep.tile([128, 1], F32, name="one")
+        dummy = keep.tile([128, 1], F32, name="dummy")
+        ident = keep.tile([128, 128], F32, name="ident")
+        cf = keep.tile([128, 32], BF16, name="cf")
+        af = keep.tile([128, 32], F32, name="af")
+        nc.vector.memset(as0[:].bitcast(I32), 0)
+        nc.vector.memset(one[:], 1.0)
+        nc.vector.memset(asr[:].rearrange("p b n -> p (b n)").bitcast(I32), 0)
+        nc.vector.memset(zs[:].rearrange("p b n -> p (b n)").bitcast(I32), 0)
+        make_identity(nc, ident[:])
+
+        nc.scalar.activation(out=dummy[:], in_=one[:], func=ACT.Abs_reciprocal_sqrt)
+        for q in range(4):
+            nc.scalar.dma_start(
+                out=as0[32 * q : 32 * q + 4, :].bitcast(I32),
+                in_=models_scales[0, 4 * q : 4 * q + 4, :].bitcast(I32),
+            )
+        nc.scalar.dma_start(
+            out=cf[:].rearrange("p (b t) -> p b t", t=4),
+            in_=conf.rearrange("b (g p t) -> p (b g) t", g=2, t=4),
+        )
+
+        xr = [keep.tile([128, 4, 512], BF16, name="xr%d" % i, align_bytes=64) for i in range(8)]
+        aw = [keep.tile([128, 2048], U8, name="aw%d" % i, align_bytes=64) for i in range(4)]
+        zw = [keep.tile([128, 2, 1024], U8, name="zw%d" % i, align_bytes=64) for i in range(4)]
+
+        def load_x(b, g, t0, t1):
+            src = x[b, 512 * g : 512 * g + 512, :].rearrange("(m t) k -> m t k", t=4)
+            nc.sync.dma_start(out=xr[2 * b + g][:, t0:t1, :], in_=src[:, t0:t1, :])
+
+        def load_a(b, lo, hi):
+            nc.sync.dma_start(
+                out=aw[b][:, lo:hi].bitcast(I32), in_=models_words[b, :, lo:hi].bitcast(I32)
+            )
+
+        def load_z(b):
+            nc.sync.dma_start(
+                out=zw[b][:].rearrange("p g n -> p (g n)").bitcast(I32).rearrange("p (g n) -> p g n", g=2),
+                in_=desc_words[2 * b : 2 * b + 2].rearrange("g p n -> p g n").bitcast(I32),
+            )
+
+        load_x(0, 0, 0, 1)
+        load_x(0, 0, 1, 2)
+        load_a(0, 0, 1024)
+        load_x(0, 0, 2, 4)
+        load_x(0, 1, 0, 4)
+        load_a(0, 1024, 2048)
+        load_x(1, 0, 0, 4)
+        load_x(1, 1, 0, 4)
+        for q in range(4):
+            nc.sync.dma_start(
+                out=asr[32 * q : 32 * q + 4, :, :].rearrange("p b n -> p (b n)").bitcast(I32).rearrange("p (b n) -> p b n", b=3),
+                in_=models_scales[1:4, 4 * q : 4 * q + 4, :].rearrange("b q n -> q b n").bitcast(I32),
+            )
+        for q in range(4):
+            nc.sync.dma_start(
+                out=zs[32 * q : 32 * q + 4, :, :].rearrange("p b n -> p (b n)").bitcast(I32).rearrange("p (b n) -> p b n", b=8),
+                in_=desc_scales[:, 4 * q : 4 * q + 4, :].rearrange("b q n -> q b n").bitcast(I32),
+            )
+        load_z(0)
+        load_a(1, 0, 2048)
+        load_x(2, 0, 0, 4)
+        load_x(2, 1, 0, 4)
+        load_z(1)
+        load_a(2, 0, 2048)
+        load_x(3, 0, 0, 4)
+        load_x(3, 1, 0, 4)
+        load_z(2)
+        load_a(3, 0, 2048)
+        load_z(3)
+
+        xc = [keep.tile([128, 512], U32, name="xc%d" % i, align_bytes=64) for i in range(8)]
+        xs = [keep.tile([128, 512], U8, name="xs%d" % i, align_bytes=64) for i in range(8)]
+
+        xt_of = {}
+        xg_of = {}
+        r_of = {}
+        u_of = {}
+        p_of = {}
+        wb_of = {}
+        wc_of = {}
+        ws_of = {}
+        o_of = {}
+
+        def x_transpose(i, half):
+            xt = psum.tile([128, 512], F32, name="xt", bufs=2)
+            xt_of[i, half] = xt
+            words = xr[i][:].rearrange("p t k -> p (t k)").bitcast(F32)
+            for tl in range(2):
+                t = 2 * half + tl
+                for u in range(2):
+                    nc.tensor.transpose(
+                        xt[:, (2 * tl + u) * 128 : (2 * tl + u + 1) * 128],
+                        words[:, t * 256 + u : (t + 1) * 256 : 2],
+                        ident[:],
+                    )
+
+        def x_copy(i, half, eng):
+            xg = work.tile([128, 1024], BF16, name="xg", bufs=3, align_bytes=64)
+            xg_of[i, half] = xg
+            dst = xg[:].bitcast(F32).rearrange("p (t r u) -> p t r u", t=2, u=2)
+            src = xt_of.pop((i, half))[:].rearrange("p (t u r) -> p t r u", t=2, u=2)
+            if eng == "s":
+                nc.scalar.copy(out=dst, in_=src)
+            else:
+                nc.vector.tensor_copy(out=dst, in_=src)
+
+        def x_quant(i, half):
+            cols = slice(256 * half, 256 * half + 256)
+            nc.vector.quantize_mx(
+                out=xc[i][:, cols].bitcast(FP8X4), scales=xs[i][:, cols], in_=xg_of.pop((i, half))[:]
+            )
+
+        def bhg(s):
+            return s // 4, (s // 2) % 2, s % 2
+
+        def m1(s, t):
+            b, h, g = bhg(s)
+            i = 2 * b + g
+            r = psum.tile([128, 512], F32, name="r", bufs=4)
+            r_of[s, t] = r
+            cols = slice(t * 128, t * 128 + 128)
+            if b == 0:
+                a_sc = as0[:, 512 * h : 512 * h + 512]
+            else:
+                a_sc = asr[:, b - 1, 512 * h : 512 * h + 512]
+            nc.tensor.matmul_mx(
+                out=r[:],
+                lhsT=xc[i][:, cols].bitcast(FP8X4),
+                lhsT_scale=xs[i][:, cols],
+                rhs=aw[b][:, 1024 * h : 1024 * h + 1024].bitcast(FP4X4),
+                rhs_scale=a_sc,
+                start=True,
+                stop=True,
+            )
+
+        def s1(s, t):
+            if t == 0:
+                u_of[s] = work.tile([128, 4, 512], F32, name="u", bufs=2, align_bytes=64)
+                p_of[s] = work.tile([128, 4, 512], F32, name="p", bufs=2, align_bytes=64)
+            nc.scalar.activation(out=u_of[s][:, t, :], in_=r_of.pop((s, t))[:], func=ACT.Square)
+
+        def s2(s, t, lo=0, hi=512):
+            b, h, g = bhg(s)
+            k = (2 * b + g) * 4 + t
+            nc.scalar.activation(
+                out=p_of[s][:, t, lo:hi],
+                in_=u_of[s][:, t, lo:hi],
+                func=ACT.Abs_reciprocal_sqrt,
+                scale=af[:, k : k + 1],
+                bias=af[:, k : k + 1],
+            )
+
+        def t_sq(s, lo, hi):
+            if lo == 0:
+                wb_of[s] = work.tile([128, 512, 4], BF16, name="wb", bufs=2, align_bytes=64)
+            src = p_of[s][:, :, lo:hi].rearrange("p t (c i) -> p c t i", i=4)
+            dst = wb_of[s][:, lo:hi, :].rearrange("p (c i) t -> p c t i", i=4)
+            nc.vector.tensor_tensor(out=dst, in0=src, in1=src, op=ALU.mult)
+
+        def w_quant(s, lo, hi):
+            if lo == 0:
+                wc_of[s] = work.tile([128, 512], U32, name="wc", bufs=4, align_bytes=64)
+                ws_of[s] = work.tile([128, 512], U8, name="ws", bufs=4, align_bytes=64)
+            nc.vector.quantize_mx(
+                out=wc_of[s][:, lo:hi].bitcast(FP8X4),
+                scales=ws_of[s][:, lo:hi],
+                in_=wb_of[s][:, lo:hi, :].rearrange("p n t -> p (n t)"),
+            )
+
+        def m2(j, mt, tag, gs=(0, 1)):
+            b, h = j // 2, j % 2
+            if gs[0] == 0:
+                o_of[j, mt] = psum.tile([128, 512], F32, name=tag, bufs=4 if tag == "r" else 2)
+            cols = slice(mt * 128, mt * 128 + 128)
+            for g in gs:
+                nc.tensor.matmul_mx(
+                    out=o_of[j, mt][:],
+                    lhsT=wc_of[2 * j + g][:, cols].bitcast(FP8X4),
+                    lhsT_scale=ws_of[2 * j + g][:, cols],
+                    rhs=zw[b][:, g, :].bitcast(FP4X4),
+                    rhs_scale=zs[:, 2 * b + g, :],
+                    start=(g == 0),
+                    stop=(g == 1),
+                )
+
+        def o_store(j, mt, eng, queue):
+            b, h = j // 2, j % 2
+            ob = work.tile([128, 512], F32, name="ob", bufs=8, align_bytes=64)
+            if eng == "s":
+                nc.scalar.copy(out=ob[:], in_=o_of.pop((j, mt))[:])
+            else:
+                nc.vector.tensor_copy(out=ob[:], in_=o_of.pop((j, mt))[:])
+            row = 512 * h + 128 * mt
+            queue.dma_start(out=out[b, row : row + 128, :], in_=ob[:])
+
+        x_transpose(0, 0)
+        x_copy(0, 0, "s")
+        x_quant(0, 0)
+        x_transpose(0, 1)
+        x_copy(0, 1, "s")
+        x_quant(0, 1)
+        nc.vector.reciprocal(out=af[:], in_=cf[:])
+        nc.vector.tensor_scalar_min(af[:], af[:], 3.0e38)
+        for t in range(4):
+            m1(0, t)
+        x_transpose(1, 0)
+        x_transpose(1, 1)
+
+        x_plan = {0: [(1, 0), (1, 1), (2, 0), (2, 1)], 1: [(3, 0), (3, 1)], 2: [(4, 0), (4, 1)],
+                  3: [], 4: [(5, 0)], 5: [], 6: [(5, 1)], 7: [(6, 0)], 8: [(6, 1)], 9: [(7, 0)], 10: [(7, 1)]}
+        pieces = {}
+        for j in range(8):
+            pieces.setdefault(2 * j + 3, []).extend([(j, 0), (j, 1)])
+            pieces.setdefault(2 * j + 4, []).extend([(j, 2), (j, 3)])
+
+        for s in range(16):
+            if s > 0:
+                for t in range(4):
+                    m1(s, t)
+            ps = pieces.get(s, [])
+            for j, mt in ps:
+                m2(j, mt, "o")
+            xp = x_plan.get(s, [])
+            for i, half in xp:
+                if i != 1:
+                    if len(xp) < 3:
+                        x_transpose(i, half)
+            for t in range(4):
+                s1(s, t)
+            if s < 15:
+                for t in range(4):
+                    s2(s, t)
+            else:
+                for lo in (0, 256):
+                    for t in range(4):
+                        s2(s, t, lo, lo + 256)
+            if s > 0:
+                t_sq(s - 1, 0, 256)
+                if ps:
+                    o_store(ps[0][0], ps[0][1], "v", nc.sync)
+                t_sq(s - 1, 256, 512)
+                if ps:
+                    o_store(ps[1][0], ps[1][1], "v", nc.sync)
+                w_quant(s - 1, 0, 512)
+            for n, (i, half) in enumerate(xp):
+                if len(xp) >= 3 and i != 1:
+                    x_transpose(i, half)
+                x_copy(i, half, "v")
+                x_quant(i, half)
+
+        for j, mt in pieces[16]:
+            m2(j, mt, "o")
+        for mt in range(4):
+            m2(7, mt, "r", (0,))
+        t_sq(15, 0, 256)
+        for j, mt in pieces[16]:
+            o_store(j, mt, "s", nc.sync)
+        w_quant(15, 0, 256)
+        t_sq(15, 256, 512)
+        m2(7, 0, "r", (1,))
+        m2(7, 1, "r", (1,))
+        o_store(7, 0, "s", nc.sync)
+        o_store(7, 1, "s", nc.sync)
+        w_quant(15, 256, 512)
+        m2(7, 2, "r", (1,))
+        m2(7, 3, "r", (1,))
+        o_store(7, 2, "s", nc.sync)
+        o_store(7, 3, "v", nc.scalar)

@@ -16,6 +16,9 @@ FP4X4 = mybir.dt.float4_e2m1fn_x4
 ACT = mybir.ActivationFunctionType
 ALU = mybir.AluOpType
 
+V_HALF, V_END, G_FROM = 256, 512, 512
+T15, T16, T17 = "ss", "  ss", "svsv"
+
 
 def tile_cauchy_hypothesis_pooling_s14_kernel(
     tc, x, models_words, models_scales, conf, desc_words, desc_scales, out
@@ -72,8 +75,8 @@ def tile_cauchy_hypothesis_pooling_s14_kernel(
             )
 
         load_x(0, 0, 0, 1)
-        load_x(0, 0, 1, 2)
         load_a(0, 0, 1024)
+        load_x(0, 0, 1, 2)
         load_x(0, 0, 2, 4)
         load_x(0, 1, 0, 4)
         load_a(0, 1024, 2048)
@@ -114,33 +117,34 @@ def tile_cauchy_hypothesis_pooling_s14_kernel(
         ws_of = {}
         o_of = {}
 
-        def x_transpose(i, half):
+        def x_transpose(i, t0, t1):
             xt = psum.tile([128, 512], F32, name="xt", bufs=2)
-            xt_of[i, half] = xt
+            xt_of[i, t0] = xt
             words = xr[i][:].rearrange("p t k -> p (t k)").bitcast(F32)
-            for tl in range(2):
-                t = 2 * half + tl
+            for t in range(t0, t1):
                 for u in range(2):
+                    c = (2 * (t - t0) + u) * 128
                     nc.tensor.transpose(
-                        xt[:, (2 * tl + u) * 128 : (2 * tl + u + 1) * 128],
-                        words[:, t * 256 + u : (t + 1) * 256 : 2],
-                        ident[:],
+                        xt[:, c : c + 128], words[:, t * 256 + u : (t + 1) * 256 : 2], ident[:]
                     )
 
-        def x_copy(i, half, eng):
+        def x_copy(i, t0, t1, eng):
+            n = 256 * (t1 - t0)
             xg = work.tile([128, 1024], BF16, name="xg", bufs=3, align_bytes=64)
-            xg_of[i, half] = xg
-            dst = xg[:].bitcast(F32).rearrange("p (t r u) -> p t r u", t=2, u=2)
-            src = xt_of.pop((i, half))[:].rearrange("p (t u r) -> p t r u", t=2, u=2)
+            xg_of[i, t0] = xg
+            dst = xg[:].bitcast(F32)[:, 0:n].rearrange("p (t r u) -> p t r u", r=128, u=2)
+            src = xt_of.pop((i, t0))[:, 0:n].rearrange("p (t u r) -> p t r u", r=128, u=2)
             if eng == "s":
                 nc.scalar.copy(out=dst, in_=src)
             else:
                 nc.vector.tensor_copy(out=dst, in_=src)
 
-        def x_quant(i, half):
-            cols = slice(256 * half, 256 * half + 256)
+        def x_quant(i, t0, t1):
+            cols = slice(128 * t0, 128 * t1)
             nc.vector.quantize_mx(
-                out=xc[i][:, cols].bitcast(FP8X4), scales=xs[i][:, cols], in_=xg_of.pop((i, half))[:]
+                out=xc[i][:, cols].bitcast(FP8X4),
+                scales=xs[i][:, cols],
+                in_=xg_of.pop((i, t0))[:, 0 : 512 * (t1 - t0)],
             )
 
         def bhg(s):
@@ -183,15 +187,15 @@ def tile_cauchy_hypothesis_pooling_s14_kernel(
                 bias=af[:, k : k + 1],
             )
 
-        def t_sq(s, lo, hi):
-            if lo == 0:
+        def t_sq(s, lo, hi, eng=nc.vector):
+            if s not in wb_of:
                 wb_of[s] = work.tile([128, 512, 4], BF16, name="wb", bufs=2, align_bytes=64)
-            src = p_of[s][:, :, lo:hi].rearrange("p t (c i) -> p c t i", i=4)
-            dst = wb_of[s][:, lo:hi, :].rearrange("p (c i) t -> p c t i", i=4)
-            nc.vector.tensor_tensor(out=dst, in0=src, in1=src, op=ALU.mult)
+            src = p_of[s][:, :, lo:hi].rearrange("p t (c i) -> p c t i", i=2)
+            dst = wb_of[s][:, lo:hi, :].rearrange("p (c i) t -> p c t i", i=2)
+            eng.tensor_tensor(out=dst, in0=src, in1=src, op=ALU.mult)
 
         def w_quant(s, lo, hi):
-            if lo == 0:
+            if s not in wc_of:
                 wc_of[s] = work.tile([128, 512], U32, name="wc", bufs=4, align_bytes=64)
                 ws_of[s] = work.tile([128, 512], U8, name="ws", bufs=4, align_bytes=64)
             nc.vector.quantize_mx(
@@ -226,76 +230,142 @@ def tile_cauchy_hypothesis_pooling_s14_kernel(
             row = 512 * h + 128 * mt
             queue.dma_start(out=out[b, row : row + 128, :], in_=ob[:])
 
-        x_transpose(0, 0)
-        x_copy(0, 0, "s")
-        x_quant(0, 0)
-        x_transpose(0, 1)
-        x_copy(0, 1, "s")
-        x_quant(0, 1)
+        x_transpose(0, 0, 1)
+        x_copy(0, 0, 1, "s")
+        x_quant(0, 0, 1)
+        x_transpose(0, 1, 2)
+        m1(0, 0)
+        x_copy(0, 1, 2, "v")
+        s1(0, 0)
+        x_transpose(0, 2, 3)
+        x_quant(0, 1, 2)
+        m1(0, 1)
+        x_copy(0, 2, 3, "v")
+        x_transpose(0, 3, 4)
+        s1(0, 1)
+        x_quant(0, 2, 3)
+        m1(0, 2)
+        x_copy(0, 3, 4, "v")
+        s1(0, 2)
+        x_quant(0, 3, 4)
+        m1(0, 3)
+        s1(0, 3)
         nc.vector.reciprocal(out=af[:], in_=cf[:])
         nc.vector.tensor_scalar_min(af[:], af[:], 3.0e38)
-        for t in range(4):
-            m1(0, t)
-        x_transpose(1, 0)
-        x_transpose(1, 1)
 
-        x_plan = {0: [(1, 0), (1, 1), (2, 0), (2, 1)], 1: [(3, 0), (3, 1)], 2: [(4, 0), (4, 1)],
-                  3: [], 4: [(5, 0)], 5: [], 6: [(5, 1)], 7: [(6, 0)], 8: [(6, 1)], 9: [(7, 0)], 10: [(7, 1)]}
+        x_early = {0: [(1, 0), (1, 2)]}
+        x_late = {1: [(3, 0), (3, 2)], 2: [(4, 0), (4, 2)],
+                  4: [(5, 0)], 6: [(5, 2)], 7: [(6, 0)], 8: [(6, 2)], 9: [(7, 0)], 10: [(7, 2)]}
+        s_copies = set()
         pieces = {}
         for j in range(8):
             pieces.setdefault(2 * j + 3, []).extend([(j, 0), (j, 1)])
             pieces.setdefault(2 * j + 4, []).extend([(j, 2), (j, 3)])
 
-        for s in range(16):
-            if s > 0:
+        def x_half(i, t0):
+            x_transpose(i, t0, t0 + 2)
+            x_copy(i, t0, t0 + 2, "v")
+            x_quant(i, t0, t0 + 2)
+
+        for s in range(15):
+            if s == 1:
+                m1(1, 0)
+                m1(1, 1)
+                x_half(2, 0)
+                m1(1, 2)
+                m1(1, 3)
+                x_half(2, 2)
+            elif s > 1:
                 for t in range(4):
                     m1(s, t)
             ps = pieces.get(s, [])
             for j, mt in ps:
                 m2(j, mt, "o")
-            xp = x_plan.get(s, [])
-            for i, half in xp:
-                if i != 1:
-                    if len(xp) < 3:
-                        x_transpose(i, half)
-            for t in range(4):
-                s1(s, t)
-            if s < 15:
-                for t in range(4):
-                    s2(s, t)
-            else:
-                for lo in (0, 256):
-                    for t in range(4):
-                        s2(s, t, lo, lo + 256)
             if s > 0:
-                t_sq(s - 1, 0, 256)
-                if ps:
-                    o_store(ps[0][0], ps[0][1], "v", nc.sync)
-                t_sq(s - 1, 256, 512)
-                if ps:
-                    o_store(ps[1][0], ps[1][1], "v", nc.sync)
+                for t in range(4):
+                    s1(s, t)
+            s_o = [p for p in ps if p in s_copies]
+            v_o = [p for p in ps if p not in s_copies]
+            s2(s, 0)
+            s2(s, 1)
+            for p in s_o:
+                o_store(p[0], p[1], "s", nc.sync)
+            s2(s, 2)
+            s2(s, 3)
+            for i, t0 in x_early.get(s, []):
+                x_half(i, t0)
+            if s == 0:
+                continue
+            t_sq(s - 1, 0, V_HALF)
+            if v_o:
+                o_store(v_o[0][0], v_o[0][1], "v", nc.sync)
+            t_sq(s - 1, V_HALF, V_END)
+            if G_FROM < 512:
+                t_sq(s - 1, G_FROM, 512, nc.gpsimd)
+            if len(v_o) > 1:
+                o_store(v_o[1][0], v_o[1][1], "v", nc.sync)
+            xp = x_late.get(s, [])
+            for n, (i, t0) in enumerate(xp):
+                x_transpose(i, t0, t0 + 2)
+                x_copy(i, t0, t0 + 2, "v")
+                if n == 0:
+                    w_quant(s - 1, 0, 512)
+                x_quant(i, t0, t0 + 2)
+            if not xp:
                 w_quant(s - 1, 0, 512)
-            for n, (i, half) in enumerate(xp):
-                if len(xp) >= 3 and i != 1:
-                    x_transpose(i, half)
-                x_copy(i, half, "v")
-                x_quant(i, half)
 
-        for j, mt in pieces[16]:
+        for t in range(4):
+            m1(15, t)
+        for j, mt in pieces[15]:
             m2(j, mt, "o")
+        slices = ((0, 256), (256, 384), (384, 512))
+        pl = [keep.tile([128, 4, hi - lo], F32, name="pl%d" % lo, align_bytes=64) for lo, hi in slices]
+        ul = keep.tile([128, 4, 512], F32, name="ul", align_bytes=64)
+        b, h, g = 3, 1, 1
+        rs = [r_of.pop((15, t)) for t in range(4)]
+        for lo, hi in ((0, 256), (256, 512)):
+            for t in range(4):
+                nc.scalar.activation(out=ul[:, t, lo:hi], in_=rs[t][:, lo:hi], func=ACT.Square)
+            for n, (l2, h2) in enumerate(slices):
+                if l2 >= lo and h2 <= hi:
+                    for t in range(4):
+                        k = 28 + t
+                        nc.scalar.activation(
+                            out=pl[n][:, t, :],
+                            in_=ul[:, t, l2:h2],
+                            func=ACT.Abs_reciprocal_sqrt,
+                            scale=af[:, k : k + 1],
+                            bias=af[:, k : k + 1],
+                        )
+        wb = work.tile([128, 512, 4], BF16, name="wb", bufs=2, align_bytes=64)
+        wb_of[15] = wb
+
+        def t_last(n):
+            lo, hi = slices[n]
+            src = pl[n][:].rearrange("p t (c i) -> p c t i", i=2)
+            dst = wb[:, lo:hi, :].rearrange("p (c i) t -> p c t i", i=2)
+            nc.vector.tensor_tensor(out=dst, in0=src, in1=src, op=ALU.mult)
+
+        t_sq(14, 0, 256)
+        t_sq(14, 256, 512)
+        for j, mt in pieces[15]:
+            o_store(j, mt, T15[mt], nc.sync)
+        w_quant(14, 0, 512)
+        for j, mt in pieces[16]:
+            m2(j, mt, "xt")
         for mt in range(4):
             m2(7, mt, "r", (0,))
-        t_sq(15, 0, 256)
+        t_last(0)
         for j, mt in pieces[16]:
-            o_store(j, mt, "s", nc.sync)
+            o_store(j, mt, T16[mt], nc.sync)
+        t_last(1)
         w_quant(15, 0, 256)
-        t_sq(15, 256, 512)
         m2(7, 0, "r", (1,))
         m2(7, 1, "r", (1,))
-        o_store(7, 0, "s", nc.sync)
-        o_store(7, 1, "s", nc.sync)
-        w_quant(15, 256, 512)
+        t_last(2)
+        w_quant(15, 256, 384)
         m2(7, 2, "r", (1,))
+        w_quant(15, 384, 512)
         m2(7, 3, "r", (1,))
-        o_store(7, 2, "s", nc.sync)
-        o_store(7, 3, "v", nc.scalar)
+        for mt in range(4):
+            o_store(7, mt, T17[mt], nc.sync if mt < 3 else nc.scalar)

@@ -16,8 +16,7 @@ FP4X4 = mybir.dt.float4_e2m1fn_x4
 ACT = mybir.ActivationFunctionType
 ALU = mybir.AluOpType
 
-V_HALF, V_END, G_FROM = 256, 512, 512
-T15, T16, T17 = "ss", "  ss", "svsv"
+T15, T16, T17 = "vs", "  ss", "svsv"
 
 
 def tile_cauchy_hypothesis_pooling_s14_kernel(
@@ -118,7 +117,7 @@ def tile_cauchy_hypothesis_pooling_s14_kernel(
         o_of = {}
 
         def x_transpose(i, t0, t1):
-            xt = psum.tile([128, 512], F32, name="xt", bufs=2)
+            xt = psum.tile([128, 512], F32, name="m", bufs=4)
             xt_of[i, t0] = xt
             words = xr[i][:].rearrange("p t k -> p (t k)").bitcast(F32)
             for t in range(t0, t1):
@@ -173,15 +172,15 @@ def tile_cauchy_hypothesis_pooling_s14_kernel(
         def s1(s, t):
             if t == 0:
                 u_of[s] = work.tile([128, 4, 512], F32, name="u", bufs=2, align_bytes=64)
-                p_of[s] = work.tile([128, 4, 512], F32, name="p", bufs=2, align_bytes=64)
+                p_of[s] = work.tile([128, 128, 4, 4], F32, name="p", bufs=2, align_bytes=64)
             nc.scalar.activation(out=u_of[s][:, t, :], in_=r_of.pop((s, t))[:], func=ACT.Square)
 
         def s2(s, t, lo=0, hi=512):
             b, h, g = bhg(s)
             k = (2 * b + g) * 4 + t
             nc.scalar.activation(
-                out=p_of[s][:, t, lo:hi],
-                in_=u_of[s][:, t, lo:hi],
+                out=p_of[s][:, lo // 4 : hi // 4, t, :],
+                in_=u_of[s][:, t, lo:hi].rearrange("p (c i) -> p c i", i=4),
                 func=ACT.Abs_reciprocal_sqrt,
                 scale=af[:, k : k + 1],
                 bias=af[:, k : k + 1],
@@ -190,8 +189,8 @@ def tile_cauchy_hypothesis_pooling_s14_kernel(
         def t_sq(s, lo, hi, eng=nc.vector):
             if s not in wb_of:
                 wb_of[s] = work.tile([128, 512, 4], BF16, name="wb", bufs=2, align_bytes=64)
-            src = p_of[s][:, :, lo:hi].rearrange("p t (c i) -> p c t i", i=2)
-            dst = wb_of[s][:, lo:hi, :].rearrange("p (c i) t -> p c t i", i=2)
+            src = p_of[s][:, lo // 4 : hi // 4, :, :]
+            dst = wb_of[s][:, lo:hi, :].rearrange("p (c i) t -> p c t i", i=4)
             eng.tensor_tensor(out=dst, in0=src, in1=src, op=ALU.mult)
 
         def w_quant(s, lo, hi):
@@ -207,7 +206,7 @@ def tile_cauchy_hypothesis_pooling_s14_kernel(
         def m2(j, mt, tag, gs=(0, 1)):
             b, h = j // 2, j % 2
             if gs[0] == 0:
-                o_of[j, mt] = psum.tile([128, 512], F32, name=tag, bufs=4 if tag == "r" else 2)
+                o_of[j, mt] = psum.tile([128, 512], F32, name=tag, bufs=4)
             cols = slice(mt * 128, mt * 128 + 128)
             for g in gs:
                 nc.tensor.matmul_mx(
@@ -256,7 +255,7 @@ def tile_cauchy_hypothesis_pooling_s14_kernel(
         x_early = {0: [(1, 0), (1, 2)]}
         x_late = {1: [(3, 0), (3, 2)], 2: [(4, 0), (4, 2)],
                   4: [(5, 0)], 6: [(5, 2)], 7: [(6, 0)], 8: [(6, 2)], 9: [(7, 0)], 10: [(7, 2)]}
-        s_copies = set()
+        s_copies = {(1, 1), (3, 1), (5, 1)}
         pieces = {}
         for j in range(8):
             pieces.setdefault(2 * j + 3, []).extend([(j, 0), (j, 1)])
@@ -280,7 +279,7 @@ def tile_cauchy_hypothesis_pooling_s14_kernel(
                     m1(s, t)
             ps = pieces.get(s, [])
             for j, mt in ps:
-                m2(j, mt, "o")
+                m2(j, mt, "m")
             if s > 0:
                 for t in range(4):
                     s1(s, t)
@@ -288,22 +287,17 @@ def tile_cauchy_hypothesis_pooling_s14_kernel(
             v_o = [p for p in ps if p not in s_copies]
             s2(s, 0)
             s2(s, 1)
-            for p in s_o:
-                o_store(p[0], p[1], "s", nc.sync)
             s2(s, 2)
             s2(s, 3)
+            for p in s_o:
+                o_store(p[0], p[1], "s", nc.sync)
             for i, t0 in x_early.get(s, []):
                 x_half(i, t0)
             if s == 0:
                 continue
-            t_sq(s - 1, 0, V_HALF)
-            if v_o:
-                o_store(v_o[0][0], v_o[0][1], "v", nc.sync)
-            t_sq(s - 1, V_HALF, V_END)
-            if G_FROM < 512:
-                t_sq(s - 1, G_FROM, 512, nc.gpsimd)
-            if len(v_o) > 1:
-                o_store(v_o[1][0], v_o[1][1], "v", nc.sync)
+            t_sq(s - 1, 0, 512)
+            for p in v_o:
+                o_store(p[0], p[1], "v", nc.sync)
             xp = x_late.get(s, [])
             for n, (i, t0) in enumerate(xp):
                 x_transpose(i, t0, t0 + 2)
@@ -317,9 +311,9 @@ def tile_cauchy_hypothesis_pooling_s14_kernel(
         for t in range(4):
             m1(15, t)
         for j, mt in pieces[15]:
-            m2(j, mt, "o")
+            m2(j, mt, "m")
         slices = ((0, 256), (256, 384), (384, 512))
-        pl = [keep.tile([128, 4, hi - lo], F32, name="pl%d" % lo, align_bytes=64) for lo, hi in slices]
+        pl = [keep.tile([128, (hi - lo) // 4, 4, 4], F32, name="pl%d" % lo, align_bytes=64) for lo, hi in slices]
         ul = keep.tile([128, 4, 512], F32, name="ul", align_bytes=64)
         b, h, g = 3, 1, 1
         rs = [r_of.pop((15, t)) for t in range(4)]
@@ -331,8 +325,8 @@ def tile_cauchy_hypothesis_pooling_s14_kernel(
                     for t in range(4):
                         k = 28 + t
                         nc.scalar.activation(
-                            out=pl[n][:, t, :],
-                            in_=ul[:, t, l2:h2],
+                            out=pl[n][:, :, t, :],
+                            in_=ul[:, t, l2:h2].rearrange("p (c i) -> p c i", i=4),
                             func=ACT.Abs_reciprocal_sqrt,
                             scale=af[:, k : k + 1],
                             bias=af[:, k : k + 1],
@@ -342,17 +336,16 @@ def tile_cauchy_hypothesis_pooling_s14_kernel(
 
         def t_last(n):
             lo, hi = slices[n]
-            src = pl[n][:].rearrange("p t (c i) -> p c t i", i=2)
-            dst = wb[:, lo:hi, :].rearrange("p (c i) t -> p c t i", i=2)
+            src = pl[n][:]
+            dst = wb[:, lo:hi, :].rearrange("p (c i) t -> p c t i", i=4)
             nc.vector.tensor_tensor(out=dst, in0=src, in1=src, op=ALU.mult)
 
-        t_sq(14, 0, 256)
-        t_sq(14, 256, 512)
+        t_sq(14, 0, 512)
         for j, mt in pieces[15]:
             o_store(j, mt, T15[mt], nc.sync)
         w_quant(14, 0, 512)
         for j, mt in pieces[16]:
-            m2(j, mt, "xt")
+            m2(j, mt, "m")
         for mt in range(4):
             m2(7, mt, "r", (0,))
         t_last(0)

from contextlib import ExitStack

import concourse.mybir as mybir
from concourse.masks import make_identity

G, C, D, H, P = 4, 1024, 512, 1024, 512
FLOPS = 2 * G * C * D * H + 2 * G * C * H * P

F32 = mybir.dt.float32
BF16 = mybir.dt.bfloat16
I32 = mybir.dt.int32
U32 = mybir.dt.uint32
U8 = mybir.dt.uint8
FP8X4 = mybir.dt.float8_e4m3fn_x4
FP4X4 = mybir.dt.float4_e2m1fn_x4
ACT = mybir.ActivationFunctionType
ALU = mybir.AluOpType

T15, T16, T17 = "vs", "  ss", "svsv"


def tile_cauchy_hypothesis_pooling_s14_kernel(
    tc, x, models_words, models_scales, conf, desc_words, desc_scales, out
):
    nc = tc.nc
    with ExitStack() as ctx:
        keep = ctx.enter_context(tc.tile_pool(name="keep", bufs=1))
        work = ctx.enter_context(tc.tile_pool(name="work", bufs=2))
        psum = ctx.enter_context(tc.psum_pool(name="psum", bufs=1))
        ctx.enter_context(tc.manual_schedule())

        as0 = keep.tile([128, 1024], U8, name="as0", align_bytes=64)
        asr = keep.tile([128, 3, 1024], U8, name="asr", align_bytes=64)
        zs = keep.tile([128, 8, 512], U8, name="zs", align_bytes=64)
        one = keep.tile([128, 1], F32, name="one")
        dummy = keep.tile([128, 1], F32, name="dummy")
        ident = keep.tile([128, 128], F32, name="ident")
        cf = keep.tile([128, 32], BF16, name="cf")
        af = keep.tile([128, 32], F32, name="af")
        nc.vector.memset(as0[:].bitcast(I32), 0)
        nc.vector.memset(one[:], 1.0)
        nc.vector.memset(asr[:].rearrange("p b n -> p (b n)").bitcast(I32), 0)
        nc.vector.memset(zs[:].rearrange("p b n -> p (b n)").bitcast(I32), 0)
        make_identity(nc, ident[:])

        nc.scalar.activation(out=dummy[:], in_=one[:], func=ACT.Abs_reciprocal_sqrt)
        for q in range(4):
            nc.scalar.dma_start(
                out=as0[32 * q : 32 * q + 4, :].bitcast(I32),
                in_=models_scales[0, 4 * q : 4 * q + 4, :].bitcast(I32),
            )
        nc.scalar.dma_start(
            out=cf[:].rearrange("p (b t) -> p b t", t=4),
            in_=conf.rearrange("b (g p t) -> p (b g) t", g=2, t=4),
        )

        xr = [keep.tile([128, 4, 512], BF16, name="xr%d" % i, align_bytes=64) for i in range(8)]
        aw = [keep.tile([128, 2048], U8, name="aw%d" % i, align_bytes=64) for i in range(4)]
        zw = [keep.tile([128, 2, 1024], U8, name="zw%d" % i, align_bytes=64) for i in range(4)]

        def load_x(b, g, t0, t1):
            src = x[b, 512 * g : 512 * g + 512, :].rearrange("(m t) k -> m t k", t=4)
            nc.sync.dma_start(out=xr[2 * b + g][:, t0:t1, :], in_=src[:, t0:t1, :])

        def load_a(b, lo, hi):
            nc.sync.dma_start(
                out=aw[b][:, lo:hi].bitcast(I32), in_=models_words[b, :, lo:hi].bitcast(I32)
            )

        def load_z(b):
            nc.sync.dma_start(
                out=zw[b][:].rearrange("p g n -> p (g n)").bitcast(I32).rearrange("p (g n) -> p g n", g=2),
                in_=desc_words[2 * b : 2 * b + 2].rearrange("g p n -> p g n").bitcast(I32),
            )

        load_x(0, 0, 0, 1)
        load_a(0, 0, 1024)
        load_x(0, 0, 1, 2)
        load_x(0, 0, 2, 4)
        load_x(0, 1, 0, 4)
        load_a(0, 1024, 2048)
        load_x(1, 0, 0, 4)
        load_x(1, 1, 0, 4)
        for q in range(4):
            nc.sync.dma_start(
                out=asr[32 * q : 32 * q + 4, :, :].rearrange("p b n -> p (b n)").bitcast(I32).rearrange("p (b n) -> p b n", b=3),
                in_=models_scales[1:4, 4 * q : 4 * q + 4, :].rearrange("b q n -> q b n").bitcast(I32),
            )
        for q in range(4):
            nc.sync.dma_start(
                out=zs[32 * q : 32 * q + 4, :, :].rearrange("p b n -> p (b n)").bitcast(I32).rearrange("p (b n) -> p b n", b=8),
                in_=desc_scales[:, 4 * q : 4 * q + 4, :].rearrange("b q n -> q b n").bitcast(I32),
            )
        load_z(0)
        load_a(1, 0, 2048)
        load_x(2, 0, 0, 4)
        load_x(2, 1, 0, 4)
        load_z(1)
        load_a(2, 0, 2048)
        load_x(3, 0, 0, 4)
        load_x(3, 1, 0, 4)
        load_z(2)
        load_a(3, 0, 2048)
        load_z(3)

        xc = [keep.tile([128, 512], U32, name="xc%d" % i, align_bytes=64) for i in range(8)]
        xs = [keep.tile([128, 512], U8, name="xs%d" % i, align_bytes=64) for i in range(8)]

        xt_of = {}
        xg_of = {}
        r_of = {}
        u_of = {}
        p_of = {}
        wb_of = {}
        wc_of = {}
        ws_of = {}
        o_of = {}

        def x_transpose(i, t0, t1):
            xt = psum.tile([128, 512], F32, name="m", bufs=4)
            xt_of[i, t0] = xt
            words = xr[i][:].rearrange("p t k -> p (t k)").bitcast(F32)
            for t in range(t0, t1):
                for u in range(2):
                    c = (2 * (t - t0) + u) * 128
                    nc.tensor.transpose(
                        xt[:, c : c + 128], words[:, t * 256 + u : (t + 1) * 256 : 2], ident[:]
                    )

        def x_copy(i, t0, t1, eng):
            n = 256 * (t1 - t0)
            xg = work.tile([128, 1024], BF16, name="xg", bufs=3, align_bytes=64)
            xg_of[i, t0] = xg
            dst = xg[:].bitcast(F32)[:, 0:n].rearrange("p (t r u) -> p t r u", r=128, u=2)
            src = xt_of.pop((i, t0))[:, 0:n].rearrange("p (t u r) -> p t r u", r=128, u=2)
            if eng == "s":
                nc.scalar.copy(out=dst, in_=src)
            else:
                nc.vector.tensor_copy(out=dst, in_=src)

        def x_quant(i, t0, t1):
            cols = slice(128 * t0, 128 * t1)
            nc.vector.quantize_mx(
                out=xc[i][:, cols].bitcast(FP8X4),
                scales=xs[i][:, cols],
                in_=xg_of.pop((i, t0))[:, 0 : 512 * (t1 - t0)],
            )

        def bhg(s):
            return s // 4, (s // 2) % 2, s % 2

        def m1(s, t):
            b, h, g = bhg(s)
            i = 2 * b + g
            r = psum.tile([128, 512], F32, name="r", bufs=4)
            r_of[s, t] = r
            cols = slice(t * 128, t * 128 + 128)
            if b == 0:
                a_sc = as0[:, 512 * h : 512 * h + 512]
            else:
                a_sc = asr[:, b - 1, 512 * h : 512 * h + 512]
            nc.tensor.matmul_mx(
                out=r[:],
                lhsT=xc[i][:, cols].bitcast(FP8X4),
                lhsT_scale=xs[i][:, cols],
                rhs=aw[b][:, 1024 * h : 1024 * h + 1024].bitcast(FP4X4),
                rhs_scale=a_sc,
                start=True,
                stop=True,
            )

        def s1(s, t):
            if t == 0:
                u_of[s] = work.tile([128, 4, 512], F32, name="u", bufs=2, align_bytes=64)
                p_of[s] = work.tile([128, 128, 4, 4], F32, name="p", bufs=2, align_bytes=64)
            nc.scalar.activation(out=u_of[s][:, t, :], in_=r_of.pop((s, t))[:], func=ACT.Square)

        def s2(s, t, lo=0, hi=512):
            b, h, g = bhg(s)
            k = (2 * b + g) * 4 + t
            nc.scalar.activation(
                out=p_of[s][:, lo // 4 : hi // 4, t, :],
                in_=u_of[s][:, t, lo:hi].rearrange("p (c i) -> p c i", i=4),
                func=ACT.Abs_reciprocal_sqrt,
                scale=af[:, k : k + 1],
                bias=af[:, k : k + 1],
            )

        def t_sq(s, lo, hi, eng=nc.vector):
            if s not in wb_of:
                wb_of[s] = work.tile([128, 512, 4], BF16, name="wb", bufs=2, align_bytes=64)
            src = p_of[s][:, lo // 4 : hi // 4, :, :]
            dst = wb_of[s][:, lo:hi, :].rearrange("p (c i) t -> p c t i", i=4)
            eng.tensor_tensor(out=dst, in0=src, in1=src, op=ALU.mult)

        def w_quant(s, lo, hi):
            if s not in wc_of:
                wc_of[s] = work.tile([128, 512], U32, name="wc", bufs=4, align_bytes=64)
                ws_of[s] = work.tile([128, 512], U8, name="ws", bufs=4, align_bytes=64)
            nc.vector.quantize_mx(
                out=wc_of[s][:, lo:hi].bitcast(FP8X4),
                scales=ws_of[s][:, lo:hi],
                in_=wb_of[s][:, lo:hi, :].rearrange("p n t -> p (n t)"),
            )

        def m2(j, mt, tag, gs=(0, 1)):
            b, h = j // 2, j % 2
            if gs[0] == 0:
                o_of[j, mt] = psum.tile([128, 512], F32, name=tag, bufs=4)
            cols = slice(mt * 128, mt * 128 + 128)
            for g in gs:
                nc.tensor.matmul_mx(
                    out=o_of[j, mt][:],
                    lhsT=wc_of[2 * j + g][:, cols].bitcast(FP8X4),
                    lhsT_scale=ws_of[2 * j + g][:, cols],
                    rhs=zw[b][:, g, :].bitcast(FP4X4),
                    rhs_scale=zs[:, 2 * b + g, :],
                    start=(g == 0),
                    stop=(g == 1),
                )

        def o_store(j, mt, eng, queue):
            b, h = j // 2, j % 2
            ob = work.tile([128, 512], F32, name="ob", bufs=8, align_bytes=64)
            if eng == "s":
                nc.scalar.copy(out=ob[:], in_=o_of.pop((j, mt))[:])
            else:
                nc.vector.tensor_copy(out=ob[:], in_=o_of.pop((j, mt))[:])
            row = 512 * h + 128 * mt
            queue.dma_start(out=out[b, row : row + 128, :], in_=ob[:])

        x_transpose(0, 0, 1)
        x_copy(0, 0, 1, "s")
        x_quant(0, 0, 1)
        x_transpose(0, 1, 2)
        m1(0, 0)
        x_copy(0, 1, 2, "v")
        s1(0, 0)
        x_transpose(0, 2, 3)
        x_quant(0, 1, 2)
        m1(0, 1)
        x_copy(0, 2, 3, "v")
        x_transpose(0, 3, 4)
        s1(0, 1)
        x_quant(0, 2, 3)
        m1(0, 2)
        x_copy(0, 3, 4, "v")
        s1(0, 2)
        x_quant(0, 3, 4)
        m1(0, 3)
        s1(0, 3)
        nc.vector.reciprocal(out=af[:], in_=cf[:])
        nc.vector.tensor_scalar_min(af[:], af[:], 3.0e38)

        x_early = {0: [(1, 0), (1, 2)]}
        x_late = {1: [(3, 0), (3, 2)], 2: [(4, 0), (4, 2)],
                  4: [(5, 0)], 6: [(5, 2)], 7: [(6, 0)], 8: [(6, 2)], 9: [(7, 0)], 10: [(7, 2)]}
        s_copies = {(1, 1), (3, 1), (5, 1)}
        pieces = {}
        for j in range(8):
            pieces.setdefault(2 * j + 3, []).extend([(j, 0), (j, 1)])
            pieces.setdefault(2 * j + 4, []).extend([(j, 2), (j, 3)])

        def x_half(i, t0):
            x_transpose(i, t0, t0 + 2)
            x_copy(i, t0, t0 + 2, "v")
            x_quant(i, t0, t0 + 2)

        for s in range(15):
            if s == 1:
                m1(1, 0)
                m1(1, 1)
                x_half(2, 0)
                m1(1, 2)
                m1(1, 3)
                x_half(2, 2)
            elif s > 1:
                for t in range(4):
                    m1(s, t)
            ps = pieces.get(s, [])
            for j, mt in ps:
                m2(j, mt, "m")
            if s > 0:
                for t in range(4):
                    s1(s, t)
            s_o = [p for p in ps if p in s_copies]
            v_o = [p for p in ps if p not in s_copies]
            s2(s, 0)
            s2(s, 1)
            s2(s, 2)
            s2(s, 3)
            for p in s_o:
                o_store(p[0], p[1], "s", nc.sync)
            for i, t0 in x_early.get(s, []):
                x_half(i, t0)
            if s == 0:
                continue
            t_sq(s - 1, 0, 512)
            for p in v_o:
                o_store(p[0], p[1], "v", nc.sync)
            xp = x_late.get(s, [])
            for n, (i, t0) in enumerate(xp):
                x_transpose(i, t0, t0 + 2)
                x_copy(i, t0, t0 + 2, "v")
                if n == 0:
                    w_quant(s - 1, 0, 512)
                x_quant(i, t0, t0 + 2)
            if not xp:
                w_quant(s - 1, 0, 512)

        for t in range(4):
            m1(15, t)
        for j, mt in pieces[15]:
            m2(j, mt, "m")
        slices = ((0, 256), (256, 384), (384, 512))
        pl = [keep.tile([128, (hi - lo) // 4, 4, 4], F32, name="pl%d" % lo, align_bytes=64) for lo, hi in slices]
        ul = keep.tile([128, 4, 512], F32, name="ul", align_bytes=64)
        b, h, g = 3, 1, 1
        rs = [r_of.pop((15, t)) for t in range(4)]
        for lo, hi in ((0, 256), (256, 512)):
            for t in range(4):
                nc.scalar.activation(out=ul[:, t, lo:hi], in_=rs[t][:, lo:hi], func=ACT.Square)
            for n, (l2, h2) in enumerate(slices):
                if l2 >= lo and h2 <= hi:
                    for t in range(4):
                        k = 28 + t
                        nc.scalar.activation(
                            out=pl[n][:, :, t, :],
                            in_=ul[:, t, l2:h2].rearrange("p (c i) -> p c i", i=4),
                            func=ACT.Abs_reciprocal_sqrt,
                            scale=af[:, k : k + 1],
                            bias=af[:, k : k + 1],
                        )
        wb = work.tile([128, 512, 4], BF16, name="wb", bufs=2, align_bytes=64)
        wb_of[15] = wb

        def t_last(n):
            lo, hi = slices[n]
            src = pl[n][:]
            dst = wb[:, lo:hi, :].rearrange("p (c i) t -> p c t i", i=4)
            nc.vector.tensor_tensor(out=dst, in0=src, in1=src, op=ALU.mult)

        t_sq(14, 0, 512)
        for j, mt in pieces[15]:
            o_store(j, mt, T15[mt], nc.sync)
        w_quant(14, 0, 512)
        for j, mt in pieces[16]:
            m2(j, mt, "m")
        for mt in range(4):
            m2(7, mt, "r", (0,))
        t_last(0)
        for j, mt in pieces[16]:
            o_store(j, mt, T16[mt], nc.sync)
        t_last(1)
        w_quant(15, 0, 256)
        m2(7, 0, "r", (1,))
        m2(7, 1, "r", (1,))
        t_last(2)
        w_quant(15, 256, 384)
        m2(7, 2, "r", (1,))
        w_quant(15, 384, 512)
        m2(7, 3, "r", (1,))
        for mt in range(4):
            o_store(7, mt, T17[mt], nc.sync if mt < 3 else nc.scalar)
